import numpy as np
import ml_dtypes


def mxq(x, axis, fmt="e4m3"):
    dtype, down = {"e4m3": (ml_dtypes.float8_e4m3fn, 7), "e5m2": (ml_dtypes.float8_e5m2, 14)}[fmt]
    v = np.moveaxis(np.asarray(x, np.float32).astype(ml_dtypes.bfloat16).astype(np.float64), axis, -1)
    blocks = v.reshape(v.shape[:-1] + (-1, 32))
    amax = np.abs(blocks).max(-1, keepdims=True)
    byte = np.maximum(np.where(amax > 0, np.frexp(amax)[1] - 1 + 127, 0) - down, 1)
    scale = np.exp2(byte - 127.0)
    codes = (blocks / scale).astype(np.float32).astype(dtype).astype(np.float64)
    return np.moveaxis((codes * scale).reshape(v.shape), -1, axis)


WIDE = False


def mx_kscale(k):
    if not WIDE:
        return np.ones(k)
    levels = np.array([10, -10, 5, -5, 0])
    if k % 512:
        return np.exp2(np.random.permutation(np.resize(levels, k // 32))).repeat(32)
    a = np.empty((k // 512, 16))
    for p in range(k // 512):
        a[p, :8] = np.random.permutation(np.resize(levels, 8))
        for g in range(8):
            far = levels[np.abs(levels - a[p, g]) >= 10]
            a[p, g + 8] = far[np.random.randint(len(far))]
    return np.exp2(a.ravel()).repeat(32)


def f64(x):
    return np.asarray(x).astype(np.float64)


def striped8(idx):
    return np.asarray(idx).reshape(8, -1, 16).transpose(0, 2, 1).reshape(128, -1).astype(np.uint16)


def unstriped8(offs):
    return offs.reshape(8, 16, -1).transpose(0, 2, 1).reshape(8, -1).astype(np.int64)


def pick8(x, idx, run):
    r = np.arange(len(x))
    return x[r[:, None], idx[r % (8 * run) // run]]


E2M1 = np.array([0.0, 0.5, 1.0, 1.5, 2.0, 3.0, 4.0, 6.0, -0.0, -0.5, -1.0, -1.5, -2.0, -3.0, -4.0, -6.0])


def pack_weight(w, fmt):
    k, n = w.shape
    w = f64(np.asarray(w, np.float32).astype(ml_dtypes.bfloat16)).reshape(k // 32, 32, n)
    amax = np.abs(w).max(1)
    if fmt == "e4m3":
        byte = np.frexp(amax)[1] - 1 + 127 - 7
    else:
        mant, ex = np.frexp(amax / 6.0)
        byte = np.where(mant > 0.5, ex, ex - 1) + 127
    byte = np.clip(np.where(amax > 0, byte, 1), 1, 254)
    scaled = (w * np.exp2(127.0 - byte)[:, None, :]).reshape(k, n).astype(np.float32)
    by_word = np.ascontiguousarray(scaled.reshape(k // 512, 128, 4, n).transpose(0, 1, 3, 2))
    if fmt == "e4m3":
        words = by_word.astype(ml_dtypes.float8_e4m3fn).view(np.uint8)
    else:
        c = by_word.astype(ml_dtypes.float4_e2m1fn).view(np.uint8) & 0xF
        words = (c[..., 0::2] | (c[..., 1::2] << 4)).reshape(k // 512, 128, 2 * n)
    return np.ascontiguousarray(words), np.ascontiguousarray(byte.astype(np.uint8).reshape(k // 512, 16, n))


def unpack_weight(words, scales, fmt):
    g, _, n = scales.shape
    words = np.ascontiguousarray(words).reshape(g, 128, n, -1)
    if fmt == "e4m3":
        vals = words.view(ml_dtypes.float8_e4m3fn).astype(np.float64)
    else:
        nib = np.empty((g, 128, n, 4), np.uint8)
        nib[..., 0::2] = words & 0xF
        nib[..., 1::2] = words >> 4
        vals = E2M1[nib]
    vals = vals * np.repeat(np.exp2(scales.astype(np.float64) - 127.0), 8, axis=1)[..., None]
    return vals.transpose(0, 1, 3, 2).reshape(g * 512, n)


D, T, Q, I, M, E = 512, 1024, 128, 512, 512, 512


def setup_inputs():
    n = np.random.standard_normal
    idx = np.stack([np.random.permutation(T)[:I] for _ in range(8)])
    fd = mx_kscale(D)
    ft = mx_kscale(T)
    fm = mx_kscale(M)
    keysp = pack_weight(n((D, T)) / fd[:, None], "e4m3")
    return {
        "query": (n((D, Q)) * 0.25 / np.sqrt(D) * fd[:, None]).astype(np.float32),
        "keys_words": keysp[0],
        "keys_scales": keysp[1],
        "pkey": (n((D, M)) / fd[:, None]).astype(np.float32),
        "fac": (np.random.uniform(0.5, 2.0, (1, T)) * ft).astype(np.float32),
        "psz": (np.random.uniform(0.5, 2.0, (1, M)) * fm).astype(np.float32),
        "vals": (n((T, E)) / ft[:, None]).astype(np.float32),
        "pval": (n((M, E)) / fm[:, None]).astype(np.float32),
        "offs": striped8(idx),
    }


def reference(query, keys_words, keys_scales, pkey, fac, psz, vals, pval, offs):
    idx = unstriped8(offs)
    keysu = unpack_weight(keys_words, keys_scales, "e4m3")
    queryq = mxq(f64(query), 0, "e4m3")
    a = queryq.T @ keysu
    b = pick8(a, idx, 16)
    pkeyq = mxq(f64(pkey), 0, "e4m3")
    r = queryq.T @ pkeyq
    z = np.maximum(np.max(b, axis=1, keepdims=True), np.max(r, axis=1, keepdims=True))
    p = np.exp(b - z)
    x = np.exp(r - z)
    n = np.sum(p, axis=1, keepdims=True) + np.sum(x, axis=1, keepdims=True)
    w = p / n
    wf = np.zeros((Q, T))
    wf[np.arange(Q)[:, None], idx[np.arange(Q) % 128 // 16]] = w
    wg = wf * f64(fac)
    wt = wg.T
    u = x * f64(psz) / n
    ut = u.T
    wtq = mxq(wt, 0, "e4m3")
    valsq = mxq(f64(vals), 0, "e4m3")
    utq = mxq(ut, 0, "e4m3")
    pvalq = mxq(f64(pval), 0, "e4m3")
    o = wtq.T @ valsq + utq.T @ pvalq
    return o

@@ -1,0 +1,216 @@
+from contextlib import ExitStack
+
+import concourse.mybir as mybir
+from concourse.masks import make_identity
+
+D, T, Q, I, M, E = 512, 1024, 128, 512, 512, 512
+FLOPS = 2 * Q * (D * T + D * M + T * E + M * E)
+
+F32 = mybir.dt.float32
+BF16 = mybir.dt.bfloat16
+I32 = mybir.dt.int32
+U32 = mybir.dt.uint32
+U16 = mybir.dt.uint16
+U8 = mybir.dt.uint8
+FP8X4 = mybir.dt.float8_e4m3fn_x4
+ALU = mybir.AluOpType
+ACT = mybir.ActivationFunctionType
+AX = mybir.AxisListType
+
+P = 128
+PACK = 4
+KP = P * PACK
+HALF = 256
+
+
+def tile_attend_beamtree_kernel(tc, query, keys_words, keys_scales, pkey, fac, psz, vals, pval, offs, out):
+    nc = tc.nc
+    with ExitStack() as ctx:
+        sb = ctx.enter_context(tc.tile_pool(name="sb", bufs=1))
+        ps = ctx.enter_context(tc.psum_pool(name="ps", bufs=1))
+
+        def tile(name, shape, dtype, tag=None):
+            return sb.tile(shape, dtype, name=name, tag=tag or name, align_bytes=64)
+
+        def bank(name, tag, shape):
+            return ps.tile(shape, F32, name=name, tag=tag)
+
+        def load_rows(name, rows, c0, c1):
+            raw = tile(name, [P, PACK, c1 - c0], F32)
+            nc.sync.dma_start(out=raw[:], in_=rows.rearrange("(p j) w -> p j w", j=PACK)[:, :, c0:c1])
+            return raw
+
+        def weave(copy, grouped, g0, raw, c0, c1):
+            dst = grouped[:, PACK * g0 : PACK * (g0 + c1 - c0)].rearrange("p (c i j) -> p c j i", i=4, j=PACK)
+            src = raw[:, :, c0:c1].rearrange("p j (c i) -> p c j i", i=4)
+            copy(out=dst, in_=src)
+
+        def quantise(name, grouped, width):
+            codes = tile(name + "_codes", [P, width], U32)
+            scales = tile(name + "_scales", [P, width], U8)
+            nc.vector.quantize_mx(out=codes[:].bitcast(FP8X4), scales=scales[:], in_=grouped[:])
+            return codes, scales
+
+        def product(acc, stat, mov, c0, c1, start, stop):
+            nc.tensor.matmul_mx(
+                out=acc,
+                lhsT=stat[0][:].bitcast(FP8X4),
+                lhsT_scale=stat[1][:],
+                rhs=mov[0][:, c0:c1].bitcast(FP8X4),
+                rhs_scale=mov[1][:, c0:c1],
+                start=start,
+                stop=stop,
+            )
+
+        offsets = sb.tile([P, I // 16], U16, name="offsets")
+        k_scales = tile("k_scales", [P, T], U8)
+        nc.gpsimd.memset(k_scales[:].bitcast(U32), 0)
+        warm = tile("warm", [P, 2], F32)
+        nc.vector.memset(warm[:, 0:1], 0.0)
+        placed = tile("placed", [P, T], F32)
+        nc.vector.memset(placed[:], 0.0)
+        nc.scalar.activation(out=warm[:, 1:2], in_=warm[:, 0:1], func=ACT.Exp)
+
+        words = keys_words[0].rearrange("p n t -> p (n t)")
+
+        def load_keys(h):
+            kc = tile("k_codes%d" % h, [P, KP], U32)
+            nc.sync.dma_start(out=kc[:].bitcast(I32), in_=words[:, h * KP * 4 : (h + 1) * KP * 4].bitcast(I32))
+            return kc
+
+        q_raw = load_rows("q_raw", query, 0, Q)
+        k_codes = [load_keys(0)]
+        for quad in range(4):
+            nc.sync.dma_start(
+                out=k_scales[32 * quad : 32 * quad + 4, :].bitcast(I32),
+                in_=keys_scales[0, 4 * quad : 4 * quad + 4, :].bitcast(I32),
+            )
+        k_codes.append(load_keys(1))
+        nc.sync.dma_start(offsets[:], offs)
+        pk_raw = [load_rows("pk_raw%d" % h, pkey, h * HALF, (h + 1) * HALF) for h in range(2)]
+        pv_raw = [load_rows("pv_raw%d" % h, pval, h * HALF, (h + 1) * HALF) for h in range(2)]
+        fac_col = tile("fac_col", [P, 2, PACK], F32)
+        nc.sync.dma_start(out=fac_col[:], in_=fac[0].rearrange("(g p j) -> p g j", g=2, j=PACK))
+        psz_col = tile("psz_col", [P, PACK], F32)
+        nc.sync.dma_start(out=psz_col[:], in_=psz[0].rearrange("(p j) -> p j", j=PACK))
+        v0_raw = [load_rows("v0_raw%d" % h, vals[0:KP, :], h * HALF, (h + 1) * HALF) for h in range(2)]
+        v1_raw = [load_rows("v1_raw%d" % h, vals[KP:T, :], h * HALF, (h + 1) * HALF) for h in range(2)]
+
+        ident = tile("ident", [P, P], F32)
+        make_identity(nc, ident[:])
+
+        q_grp = tile("q_grp", [P, PACK * Q], BF16)
+        weave(nc.vector.tensor_copy, q_grp, 0, q_raw, 0, Q)
+        q_mx = quantise("q", q_grp, Q)
+        scores = tile("scores", [P, T], F32)
+        for c in range(4):
+            acc = bank("a%d" % c, "A%d" % c, [P, HALF])
+            h, c0 = divmod(c * HALF, KP)
+            nc.tensor.matmul_mx(
+                out=acc[:],
+                lhsT=q_mx[0][:].bitcast(FP8X4),
+                lhsT_scale=q_mx[1][:],
+                rhs=k_codes[h][:, c0 : c0 + HALF].bitcast(FP8X4),
+                rhs_scale=k_scales[:, c * HALF : (c + 1) * HALF],
+                start=True,
+                stop=True,
+            )
+            copy = nc.scalar.copy if c % 2 == 0 else nc.vector.tensor_copy
+            copy(out=scores[:, c * HALF : (c + 1) * HALF], in_=acc[:])
+
+        listed = tile("listed", [P, I], F32)
+        nc.vector.tensor_copy(listed[:], scores[:].indirect(offsets[:]))
+        pk_grp = [tile("pk_grp%d" % h, [P, PACK * HALF], BF16) for h in range(2)]
+        weave(nc.scalar.copy, pk_grp[0], 0, pk_raw[0], 0, HALF)
+        weave(nc.scalar.copy, pk_grp[1], 0, pk_raw[1], 0, HALF // 2)
+        r_acc = bank("r", "R", [P, M])
+        pk_mx = quantise("pk0", pk_grp[0], HALF)
+        product(r_acc[:, 0:HALF], q_mx, pk_mx, 0, HALF, True, True)
+        weave(nc.vector.tensor_copy, pk_grp[1], HALF // 2, pk_raw[1], HALF // 2, HALF)
+        low0 = tile("low0", [P, 1], F32)
+        nc.vector.tensor_reduce(out=low0[:], in_=r_acc[:, 0:HALF], axis=AX.X, op=ALU.max, negate=True)
+        pk_mx = quantise("pk1", pk_grp[1], HALF)
+        product(r_acc[:, HALF:M], q_mx, pk_mx, 0, HALF, True, True)
+        neg_listed = tile("neg_listed", [P, I], F32)
+        low1 = tile("low1", [P, 1], F32)
+        nc.vector.tensor_scalar(
+            out=neg_listed[:], in0=listed[:], scalar1=-1.0, scalar2=low0[:], op0=ALU.mult, op1=ALU.min, accum_out=low1[:]
+        )
+        neg_r = tile("neg_r", [P, HALF], F32)
+        neg_z = tile("neg_z", [P, 1], F32)
+        nc.vector.tensor_scalar(
+            out=neg_r[:], in0=r_acc[:, HALF:M], scalar1=-1.0, scalar2=low1[:], op0=ALU.mult, op1=ALU.min, accum_out=neg_z[:]
+        )
+
+        def value_half(name, raw, copy):
+            grp = tile(name + "_grp", [P, PACK * HALF], BF16)
+            weave(copy, grp, 0, raw, 0, HALF)
+            return grp
+
+        pv_grp = [value_half("pv0", pv_raw[0], nc.scalar.copy)]
+        p = tile("p", [P, I], F32)
+        x = tile("x", [P, M], F32)
+        sums = tile("sums", [P, 3], F32)
+        nc.scalar.activation(out=p[:, 0:HALF], in_=neg_listed[:, 0:HALF], func=ACT.Exp, scale=-1.0, bias=neg_z[:], accum_out=sums[:, 0:1])
+        nc.scalar.activation(out=p[:, HALF:I], in_=neg_listed[:, HALF:I], func=ACT.Exp, scale=-1.0, bias=neg_z[:], accum_out=sums[:, 1:2])
+        nc.scalar.activation(out=x[:], in_=r_acc[:], func=ACT.Exp, bias=neg_z[:], accum_out=sums[:, 2:3])
+        pv_mx = [quantise("pv0", pv_grp[0], HALF)]
+        for h in range(2):
+            nc.vector.tensor_copy(placed[:].indirect(offsets[:, 16 * h : 16 * (h + 1)]), p[:, h * HALF : (h + 1) * HALF])
+        sums_again = tile("sums_again", [P, 3], F32)
+        total = tile("total", [P, 1], F32)
+        nc.scalar.activation(out=sums_again[:], in_=sums[:], func=ACT.Copy, accum_out=total[:])
+        inv = tile("inv", [P, 1], F32)
+        nc.vector.reciprocal(out=inv[:], in_=total[:])
+
+        spread = []
+        for g in range(3):
+            sp = bank("spread%d" % g, "S%d" % g, [P, PACK, P])
+            for j in range(PACK):
+                col = fac_col[:, g, j : j + 1] if g < 2 else psz_col[:, j : j + 1]
+                nc.tensor.transpose(sp[:, j, :], col.to_broadcast([P, P]), ident[:])
+            spread.append(sp)
+
+        pv_grp.append(value_half("pv1", pv_raw[1], nc.scalar.copy))
+        v0_grp = [value_half("v0%d" % h, v0_raw[h], nc.scalar.copy) for h in range(2)]
+        v1_grp = [value_half("v1%d" % h, v1_raw[h], nc.scalar.copy) for h in range(2)]
+
+        def weights(name, src, sp, tag, grp):
+            wb = tile(name + "_bf", [P, KP], BF16)
+            nc.vector.scalar_tensor_tensor(
+                out=wb[:].rearrange("q (p j) -> q p j", j=PACK),
+                in0=src.rearrange("q (p j) -> q p j", j=PACK),
+                scalar=inv[:],
+                in1=sp[:].rearrange("q j p -> q p j"),
+                op0=ALU.mult,
+                op1=ALU.mult,
+            )
+            pairs = wb[:].bitcast(F32)
+            turned = bank(name + "_turned", tag, [P, 2, Q])
+            for u in range(2):
+                nc.tensor.transpose(turned[:, u, :], pairs[:, u : 2 * P : 2], ident[:])
+            nc.scalar.copy(
+                out=grp.bitcast(F32).rearrange("p (q u) -> p q u", u=2), in_=turned[:].rearrange("p u q -> p q u")
+            )
+
+        pv_mx.append(quantise("pv1", pv_grp[1], HALF))
+        u_grp = tile("u_grp", [P, PACK * Q], BF16, tag="v1_raw0")
+        w_grp = tile("w_grp", [P, 2 * PACK * Q], BF16, tag="v1_raw1")
+        weights("u", x[:], spread[2], "R", u_grp[:])
+        weights("w0", placed[:, 0:KP], spread[0], "A2", w_grp[:, 0 : PACK * Q])
+        weights("w1", placed[:, KP:T], spread[1], "A3", w_grp[:, PACK * Q : 2 * PACK * Q])
+        v0_mx = [quantise("v0%d" % h, v0_grp[h], HALF) for h in range(2)]
+        u_mx = quantise("u", u_grp, Q)
+        v1_mx = [quantise("v1%d" % h, v1_grp[h], HALF) for h in range(2)]
+        w_codes, w_scales = quantise("w", w_grp, 2 * Q)
+        w_mx = [(w_codes[:, g * Q : (g + 1) * Q], w_scales[:, g * Q : (g + 1) * Q]) for g in range(2)]
+        accs = [bank("o%d" % h, "A%d" % h, [P, HALF]) for h in range(2)]
+        for h in range(2):
+            product(accs[h][:], u_mx, pv_mx[h], 0, HALF, True, False)
+        for h in range(2):
+            product(accs[h][:], w_mx[0], v0_mx[h], 0, HALF, False, False)
+            product(accs[h][:], w_mx[1], v1_mx[h], 0, HALF, False, True)
+            res = tile("res%d" % h, [P, HALF], F32)
+            copy = nc.scalar.copy if h == 0 else nc.vector.tensor_copy
+            copy(out=res[:], in_=accs[h][:])
+            nc.sync.dma_start(out=out[:, h * HALF : (h + 1) * HALF], in_=res[:])

@@ -21,6 +21,7 @@ P = 128
 PACK = 4
 KP = P * PACK
 HALF = 256
+SPLIT = 128
 
 
 def tile_attend_beamtree_kernel(tc, query, keys_words, keys_scales, pkey, fac, psz, vals, pval, offs, out):
@@ -45,8 +46,8 @@ def tile_attend_beamtree_kernel(tc, query, keys_words, keys_scales, pkey, fac, p
             src = raw[:, :, c0:c1].rearrange("p j (c i) -> p c j i", i=4)
             copy(out=dst, in_=src)
 
-        def quantise(name, grouped, width):
-            codes = tile(name + "_codes", [P, width], U32)
+        def quantise(name, grouped, width, tag=None):
+            codes = tile(name + "_codes", [P, width], U32, tag=tag)
             scales = tile(name + "_scales", [P, width], U8)
             nc.vector.quantize_mx(out=codes[:].bitcast(FP8X4), scales=scales[:], in_=grouped[:])
             return codes, scales
@@ -65,6 +66,8 @@ def tile_attend_beamtree_kernel(tc, query, keys_words, keys_scales, pkey, fac, p
         offsets = sb.tile([P, I // 16], U16, name="offsets")
         k_scales = tile("k_scales", [P, T], U8)
         nc.gpsimd.memset(k_scales[:].bitcast(U32), 0)
+        factor_rows = tile("factor_rows", [P, P], F32)
+        nc.gpsimd.memset(factor_rows[:], 0.0)
         warm = tile("warm", [P, 2], F32)
         nc.vector.memset(warm[:, 0:1], 0.0)
         placed = tile("placed", [P, T], F32)
@@ -80,20 +83,15 @@ def tile_attend_beamtree_kernel(tc, query, keys_words, keys_scales, pkey, fac, p
 
         q_raw = load_rows("q_raw", query, 0, Q)
         k_codes = [load_keys(0)]
-        for quad in range(4):
-            nc.sync.dma_start(
-                out=k_scales[32 * quad : 32 * quad + 4, :].bitcast(I32),
-                in_=keys_scales[0, 4 * quad : 4 * quad + 4, :].bitcast(I32),
-            )
+        for r in range(4):
+            nc.sync.dma_start(out=k_scales[r:P:32, :].bitcast(I32), in_=keys_scales[0, r:16:4, :].bitcast(I32))
         k_codes.append(load_keys(1))
         nc.sync.dma_start(offsets[:], offs)
         pk_raw = [load_rows("pk_raw%d" % h, pkey, h * HALF, (h + 1) * HALF) for h in range(2)]
         pv_raw = [load_rows("pv_raw%d" % h, pval, h * HALF, (h + 1) * HALF) for h in range(2)]
-        fac_col = tile("fac_col", [P, 2, PACK], F32)
-        nc.sync.dma_start(out=fac_col[:], in_=fac[0].rearrange("(g p j) -> p g j", g=2, j=PACK))
-        psz_col = tile("psz_col", [P, PACK], F32)
-        nc.sync.dma_start(out=psz_col[:], in_=psz[0].rearrange("(p j) -> p j", j=PACK))
-        v0_raw = [load_rows("v0_raw%d" % h, vals[0:KP, :], h * HALF, (h + 1) * HALF) for h in range(2)]
+        nc.sync.dma_start(out=factor_rows[0:8, :], in_=fac[0].rearrange("(m c) -> m c", c=P))
+        nc.sync.dma_start(out=factor_rows[8:12, :], in_=psz[0].rearrange("(m c) -> m c", c=P))
+        v0_raw = load_rows("v0_raw", vals[0:KP, :], 0, E)
         v1_raw = [load_rows("v1_raw%d" % h, vals[KP:T, :], h * HALF, (h + 1) * HALF) for h in range(2)]
 
         ident = tile("ident", [P, P], F32)
@@ -121,25 +119,23 @@ def tile_attend_beamtree_kernel(tc, query, keys_words, keys_scales, pkey, fac, p
         listed = tile("listed", [P, I], F32)
         nc.vector.tensor_copy(listed[:], scores[:].indirect(offsets[:]))
         pk_grp = [tile("pk_grp%d" % h, [P, PACK * HALF], BF16) for h in range(2)]
+        r_acc = bank("r", "R", [P, M])
         weave(nc.scalar.copy, pk_grp[0], 0, pk_raw[0], 0, HALF)
         weave(nc.scalar.copy, pk_grp[1], 0, pk_raw[1], 0, HALF // 2)
-        r_acc = bank("r", "R", [P, M])
         pk_mx = quantise("pk0", pk_grp[0], HALF)
         product(r_acc[:, 0:HALF], q_mx, pk_mx, 0, HALF, True, True)
         weave(nc.vector.tensor_copy, pk_grp[1], HALF // 2, pk_raw[1], HALF // 2, HALF)
-        low0 = tile("low0", [P, 1], F32)
-        nc.vector.tensor_reduce(out=low0[:], in_=r_acc[:, 0:HALF], axis=AX.X, op=ALU.max, negate=True)
         pk_mx = quantise("pk1", pk_grp[1], HALF)
         product(r_acc[:, HALF:M], q_mx, pk_mx, 0, HALF, True, True)
-        neg_listed = tile("neg_listed", [P, I], F32)
-        low1 = tile("low1", [P, 1], F32)
-        nc.vector.tensor_scalar(
-            out=neg_listed[:], in0=listed[:], scalar1=-1.0, scalar2=low0[:], op0=ALU.mult, op1=ALU.min, accum_out=low1[:]
-        )
-        neg_r = tile("neg_r", [P, HALF], F32)
+        neg_listed = tile("neg_listed", [P, I], F32, tag="pk_grp1")
+        neg_r = tile("neg_r", [P, M], F32)
+        neg_zb = tile("neg_zb", [P, 1], F32)
         neg_z = tile("neg_z", [P, 1], F32)
         nc.vector.tensor_scalar(
-            out=neg_r[:], in0=r_acc[:, HALF:M], scalar1=-1.0, scalar2=low1[:], op0=ALU.mult, op1=ALU.min, accum_out=neg_z[:]
+            out=neg_listed[:], in0=listed[:], scalar1=-1.0, scalar2=None, op0=ALU.mult, op1=ALU.min, accum_out=neg_zb[:]
+        )
+        nc.vector.tensor_scalar(
+            out=neg_r[:], in0=r_acc[:], scalar1=-1.0, scalar2=neg_zb[:], op0=ALU.mult, op1=ALU.min, accum_out=neg_z[:]
         )
 
         def value_half(name, raw, copy):
@@ -153,7 +149,7 @@ def tile_attend_beamtree_kernel(tc, query, keys_words, keys_scales, pkey, fac, p
         sums = tile("sums", [P, 3], F32)
         nc.scalar.activation(out=p[:, 0:HALF], in_=neg_listed[:, 0:HALF], func=ACT.Exp, scale=-1.0, bias=neg_z[:], accum_out=sums[:, 0:1])
         nc.scalar.activation(out=p[:, HALF:I], in_=neg_listed[:, HALF:I], func=ACT.Exp, scale=-1.0, bias=neg_z[:], accum_out=sums[:, 1:2])
-        nc.scalar.activation(out=x[:], in_=r_acc[:], func=ACT.Exp, bias=neg_z[:], accum_out=sums[:, 2:3])
+        nc.scalar.activation(out=x[:], in_=neg_r[:], func=ACT.Exp, scale=-1.0, bias=neg_z[:], accum_out=sums[:, 2:3])
         pv_mx = [quantise("pv0", pv_grp[0], HALF)]
         for h in range(2):
             nc.vector.tensor_copy(placed[:].indirect(offsets[:, 16 * h : 16 * (h + 1)]), p[:, h * HALF : (h + 1) * HALF])
@@ -163,25 +159,31 @@ def tile_attend_beamtree_kernel(tc, query, keys_words, keys_scales, pkey, fac, p
         inv = tile("inv", [P, 1], F32)
         nc.vector.reciprocal(out=inv[:], in_=total[:])
 
+        factor_turned = bank("factor_turned", "A2", [P, P])
+        nc.tensor.transpose(factor_turned[:], factor_rows[:], ident[:])
+        factor_cols = tile("factor_cols", [P, 12], F32)
+        nc.scalar.copy(out=factor_cols[:], in_=factor_turned[:, 0:12])
         spread = []
         for g in range(3):
-            sp = bank("spread%d" % g, "S%d" % g, [P, PACK, P])
-            for j in range(PACK):
-                col = fac_col[:, g, j : j + 1] if g < 2 else psz_col[:, j : j + 1]
-                nc.tensor.transpose(sp[:, j, :], col.to_broadcast([P, P]), ident[:])
+            sp = bank("spread%d" % g, "S%d" % g, [P, KP])
+            for m in range(4):
+                col = factor_cols[:, 4 * g + m : 4 * g + m + 1]
+                nc.tensor.transpose(sp[:, m * P : (m + 1) * P], col.to_broadcast([P, P]), ident[:])
             spread.append(sp)
 
         pv_grp.append(value_half("pv1", pv_raw[1], nc.scalar.copy))
-        v0_grp = [value_half("v0%d" % h, v0_raw[h], nc.scalar.copy) for h in range(2)]
-        v1_grp = [value_half("v1%d" % h, v1_raw[h], nc.scalar.copy) for h in range(2)]
+        v0_grp = tile("v0_grp", [P, PACK * E], BF16)
+        for h in range(2):
+            weave(nc.scalar.copy, v0_grp, h * HALF, v0_raw, h * HALF, (h + 1) * HALF)
+        v1_grp = [value_half("v10", v1_raw[0], nc.scalar.copy)]
 
         def weights(name, src, sp, tag, grp):
             wb = tile(name + "_bf", [P, KP], BF16)
             nc.vector.scalar_tensor_tensor(
-                out=wb[:].rearrange("q (p j) -> q p j", j=PACK),
-                in0=src.rearrange("q (p j) -> q p j", j=PACK),
+                out=wb[:],
+                in0=src,
                 scalar=inv[:],
-                in1=sp[:].rearrange("q j p -> q p j"),
+                in1=sp[:],
                 op0=ALU.mult,
                 op1=ALU.mult,
             )
@@ -194,23 +196,26 @@ def tile_attend_beamtree_kernel(tc, query, keys_words, keys_scales, pkey, fac, p
             )
 
         pv_mx.append(quantise("pv1", pv_grp[1], HALF))
-        u_grp = tile("u_grp", [P, PACK * Q], BF16, tag="v1_raw0")
-        w_grp = tile("w_grp", [P, 2 * PACK * Q], BF16, tag="v1_raw1")
-        weights("u", x[:], spread[2], "R", u_grp[:])
-        weights("w0", placed[:, 0:KP], spread[0], "A2", w_grp[:, 0 : PACK * Q])
-        weights("w1", placed[:, KP:T], spread[1], "A3", w_grp[:, PACK * Q : 2 * PACK * Q])
-        v0_mx = [quantise("v0%d" % h, v0_grp[h], HALF) for h in range(2)]
-        u_mx = quantise("u", u_grp, Q)
-        v1_mx = [quantise("v1%d" % h, v1_grp[h], HALF) for h in range(2)]
-        w_codes, w_scales = quantise("w", w_grp, 2 * Q)
-        w_mx = [(w_codes[:, g * Q : (g + 1) * Q], w_scales[:, g * Q : (g + 1) * Q]) for g in range(2)]
+        wu_grp = tile("wu_grp", [P, 3 * KP], BF16, tag="v1_raw0")
+        weights("w0", placed[:, 0:KP], spread[0], "A2", wu_grp[:, 0:KP])
+        weights("u", x[:], spread[2], "R", wu_grp[:, KP : 2 * KP])
+        weights("w1", placed[:, KP:T], spread[1], "A3", wu_grp[:, 2 * KP : 3 * KP])
+        v11_grp = tile("v11_grp", [P, PACK * HALF], BF16)
+        weave(nc.scalar.copy, v11_grp, 0, v1_raw[1], 0, SPLIT)
+        v0_mx = quantise("v0", v0_grp, E)
+        weave(nc.vector.tensor_copy, v11_grp, SPLIT, v1_raw[1], SPLIT, HALF)
         accs = [bank("o%d" % h, "A%d" % h, [P, HALF]) for h in range(2)]
+        w0_mx = quantise("w0", wu_grp[:, 0:KP], Q)
         for h in range(2):
-            product(accs[h][:], u_mx, pv_mx[h], 0, HALF, True, False)
+            product(accs[h][:], w0_mx, v0_mx, h * HALF, (h + 1) * HALF, True, False)
+        u_mx = quantise("u", wu_grp[:, KP : 2 * KP], Q)
         for h in range(2):
-            product(accs[h][:], w_mx[0], v0_mx[h], 0, HALF, False, False)
-            product(accs[h][:], w_mx[1], v1_mx[h], 0, HALF, False, True)
+            product(accs[h][:], u_mx, pv_mx[h], 0, HALF, False, False)
+        w1_mx = quantise("w1", wu_grp[:, 2 * KP : 3 * KP], Q)
+        v1_mx = [quantise("v10", v1_grp[0], HALF, tag="v1_raw0"), quantise("v11", v11_grp, HALF)]
+        for h in range(2):
+            product(accs[h][:], w1_mx, v1_mx[h], 0, HALF, False, True)
             res = tile("res%d" % h, [P, HALF], F32)
-            copy = nc.scalar.copy if h == 0 else nc.vector.tensor_copy
+            copy = nc.vector.tensor_copy if h == 0 else nc.scalar.copy
             copy(out=res[:], in_=accs[h][:])
             nc.sync.dma_start(out=out[:, h * HALF : (h + 1) * HALF], in_=res[:])

@@ -86,8 +86,9 @@ def tile_attend_beamtree_kernel(tc, query, keys_words, keys_scales, pkey, fac, p
         for r in range(4):
             nc.sync.dma_start(out=k_scales[r:P:32, :].bitcast(I32), in_=keys_scales[0, r:16:4, :].bitcast(I32))
         k_codes.append(load_keys(1))
+        pk_raw = [load_rows("pk_raw0", pkey, 0, HALF)]
         nc.sync.dma_start(offsets[:], offs)
-        pk_raw = [load_rows("pk_raw%d" % h, pkey, h * HALF, (h + 1) * HALF) for h in range(2)]
+        pk_raw.append(load_rows("pk_raw1", pkey, HALF, M))
         pv_raw = [load_rows("pv_raw%d" % h, pval, h * HALF, (h + 1) * HALF) for h in range(2)]
         nc.sync.dma_start(out=factor_rows[0:8, :], in_=fac[0].rearrange("(m c) -> m c", c=P))
         nc.sync.dma_start(out=factor_rows[8:12, :], in_=psz[0].rearrange("(m c) -> m c", c=P))
@@ -116,21 +117,18 @@ def tile_attend_beamtree_kernel(tc, query, keys_words, keys_scales, pkey, fac, p
             copy = nc.scalar.copy if c % 2 == 0 else nc.vector.tensor_copy
             copy(out=scores[:, c * HALF : (c + 1) * HALF], in_=acc[:])
 
-        listed = tile("listed", [P, I], F32)
-        nc.vector.tensor_copy(listed[:], scores[:].indirect(offsets[:]))
-        pk_grp = [tile("pk_grp%d" % h, [P, PACK * HALF], BF16) for h in range(2)]
-        r_acc = bank("r", "R", [P, M])
-        weave(nc.scalar.copy, pk_grp[0], 0, pk_raw[0], 0, HALF)
-        weave(nc.scalar.copy, pk_grp[1], 0, pk_raw[1], 0, HALF // 2)
-        pk_mx = quantise("pk0", pk_grp[0], HALF)
-        product(r_acc[:, 0:HALF], q_mx, pk_mx, 0, HALF, True, True)
-        weave(nc.vector.tensor_copy, pk_grp[1], HALF // 2, pk_raw[1], HALF // 2, HALF)
-        pk_mx = quantise("pk1", pk_grp[1], HALF)
-        product(r_acc[:, HALF:M], q_mx, pk_mx, 0, HALF, True, True)
-        neg_listed = tile("neg_listed", [P, I], F32, tag="pk_grp1")
         neg_r = tile("neg_r", [P, M], F32)
         neg_zb = tile("neg_zb", [P, 1], F32)
         neg_z = tile("neg_z", [P, 1], F32)
+        listed = tile("listed", [P, I], F32)
+        nc.vector.tensor_copy(listed[:], scores[:].indirect(offsets[:]))
+        r_acc = bank("r", "A2", [P, M])
+        pk_grp = [tile("pk_grp%d" % h, [P, PACK * HALF], BF16) for h in range(2)]
+        for h in range(2):
+            weave(nc.scalar.copy, pk_grp[h], 0, pk_raw[h], 0, HALF)
+            pk_mx = quantise("pk%d" % h, pk_grp[h], HALF)
+            product(r_acc[:, h * HALF : (h + 1) * HALF], q_mx, pk_mx, 0, HALF, True, True)
+        neg_listed = tile("neg_listed", [P, I], F32, tag="pk_grp1")
         nc.vector.tensor_scalar(
             out=neg_listed[:], in0=listed[:], scalar1=-1.0, scalar2=None, op0=ALU.mult, op1=ALU.min, accum_out=neg_zb[:]
         )
@@ -159,7 +157,7 @@ def tile_attend_beamtree_kernel(tc, query, keys_words, keys_scales, pkey, fac, p
         inv = tile("inv", [P, 1], F32)
         nc.vector.reciprocal(out=inv[:], in_=total[:])
 
-        factor_turned = bank("factor_turned", "A2", [P, P])
+        factor_turned = bank("factor_turned", "R", [P, P])
         nc.tensor.transpose(factor_turned[:], factor_rows[:], ident[:])
         factor_cols = tile("factor_cols", [P, 12], F32)
         nc.scalar.copy(out=factor_cols[:], in_=factor_turned[:, 0:12])
@@ -201,9 +199,8 @@ def tile_attend_beamtree_kernel(tc, query, keys_words, keys_scales, pkey, fac, p
         weights("u", x[:], spread[2], "R", wu_grp[:, KP : 2 * KP])
         weights("w1", placed[:, KP:T], spread[1], "A3", wu_grp[:, 2 * KP : 3 * KP])
         v11_grp = tile("v11_grp", [P, PACK * HALF], BF16)
-        weave(nc.scalar.copy, v11_grp, 0, v1_raw[1], 0, SPLIT)
+        weave(nc.scalar.copy, v11_grp, 0, v1_raw[1], 0, HALF)
         v0_mx = quantise("v0", v0_grp, E)
-        weave(nc.vector.tensor_copy, v11_grp, SPLIT, v1_raw[1], SPLIT, HALF)
         accs = [bank("o%d" % h, "A%d" % h, [P, HALF]) for h in range(2)]
         w0_mx = quantise("w0", wu_grp[:, 0:KP], Q)
         for h in range(2):
@@ -216,6 +213,6 @@ def tile_attend_beamtree_kernel(tc, query, keys_words, keys_scales, pkey, fac, p
         for h in range(2):
             product(accs[h][:], w1_mx, v1_mx[h], 0, HALF, False, True)
             res = tile("res%d" % h, [P, HALF], F32)
-            copy = nc.vector.tensor_copy if h == 0 else nc.scalar.copy
+            copy = nc.scalar.copy if h == 0 else nc.vector.tensor_copy
             copy(out=res[:], in_=accs[h][:])
             nc.sync.dma_start(out=out[:, h * HALF : (h + 1) * HALF], in_=res[:])

from contextlib import ExitStack

import concourse.mybir as mybir
from concourse.masks import make_identity

D, T, Q, I, M, E = 512, 1024, 128, 512, 512, 512
FLOPS = 2 * Q * (D * T + D * M + T * E + M * E)

F32 = mybir.dt.float32
BF16 = mybir.dt.bfloat16
I32 = mybir.dt.int32
U32 = mybir.dt.uint32
U16 = mybir.dt.uint16
U8 = mybir.dt.uint8
FP8X4 = mybir.dt.float8_e4m3fn_x4
ALU = mybir.AluOpType
ACT = mybir.ActivationFunctionType
AX = mybir.AxisListType

P = 128
PACK = 4
KP = P * PACK
HALF = 256
SPLIT = 128


def tile_attend_beamtree_kernel(tc, query, keys_words, keys_scales, pkey, fac, psz, vals, pval, offs, out):
    nc = tc.nc
    with ExitStack() as ctx:
        sb = ctx.enter_context(tc.tile_pool(name="sb", bufs=1))
        ps = ctx.enter_context(tc.psum_pool(name="ps", bufs=1))

        def tile(name, shape, dtype, tag=None):
            return sb.tile(shape, dtype, name=name, tag=tag or name, align_bytes=64)

        def bank(name, tag, shape):
            return ps.tile(shape, F32, name=name, tag=tag)

        def load_rows(name, rows, c0, c1):
            raw = tile(name, [P, PACK, c1 - c0], F32)
            nc.sync.dma_start(out=raw[:], in_=rows.rearrange("(p j) w -> p j w", j=PACK)[:, :, c0:c1])
            return raw

        def weave(copy, grouped, g0, raw, c0, c1):
            dst = grouped[:, PACK * g0 : PACK * (g0 + c1 - c0)].rearrange("p (c i j) -> p c j i", i=4, j=PACK)
            src = raw[:, :, c0:c1].rearrange("p j (c i) -> p c j i", i=4)
            copy(out=dst, in_=src)

        def quantise(name, grouped, width, tag=None):
            codes = tile(name + "_codes", [P, width], U32, tag=tag)
            scales = tile(name + "_scales", [P, width], U8)
            nc.vector.quantize_mx(out=codes[:].bitcast(FP8X4), scales=scales[:], in_=grouped[:])
            return codes, scales

        def product(acc, stat, mov, c0, c1, start, stop):
            nc.tensor.matmul_mx(
                out=acc,
                lhsT=stat[0][:].bitcast(FP8X4),
                lhsT_scale=stat[1][:],
                rhs=mov[0][:, c0:c1].bitcast(FP8X4),
                rhs_scale=mov[1][:, c0:c1],
                start=start,
                stop=stop,
            )

        offsets = sb.tile([P, I // 16], U16, name="offsets")
        k_scales = tile("k_scales", [P, T], U8)
        nc.gpsimd.memset(k_scales[:].bitcast(U32), 0)
        factor_rows = tile("factor_rows", [P, P], F32)
        nc.gpsimd.memset(factor_rows[:], 0.0)
        warm = tile("warm", [P, 2], F32)
        nc.vector.memset(warm[:, 0:1], 0.0)
        placed = tile("placed", [P, T], F32)
        nc.vector.memset(placed[:], 0.0)
        nc.scalar.activation(out=warm[:, 1:2], in_=warm[:, 0:1], func=ACT.Exp)

        words = keys_words[0].rearrange("p n t -> p (n t)")

        def load_keys(h):
            kc = tile("k_codes%d" % h, [P, KP], U32)
            nc.sync.dma_start(out=kc[:].bitcast(I32), in_=words[:, h * KP * 4 : (h + 1) * KP * 4].bitcast(I32))
            return kc

        q_raw = load_rows("q_raw", query, 0, Q)
        k_codes = [load_keys(0)]
        for r in range(4):
            nc.sync.dma_start(out=k_scales[r:P:32, :].bitcast(I32), in_=keys_scales[0, r:16:4, :].bitcast(I32))
        k_codes.append(load_keys(1))
        pk_raw = [load_rows("pk_raw0", pkey, 0, HALF)]
        nc.sync.dma_start(offsets[:], offs)
        pk_raw.append(load_rows("pk_raw1", pkey, HALF, M))
        pv_raw = [load_rows("pv_raw%d" % h, pval, h * HALF, (h + 1) * HALF) for h in range(2)]
        nc.sync.dma_start(out=factor_rows[0:8, :], in_=fac[0].rearrange("(m c) -> m c", c=P))
        nc.sync.dma_start(out=factor_rows[8:12, :], in_=psz[0].rearrange("(m c) -> m c", c=P))
        v0_raw = load_rows("v0_raw", vals[0:KP, :], 0, E)
        v1_raw = [load_rows("v1_raw%d" % h, vals[KP:T, :], h * HALF, (h + 1) * HALF) for h in range(2)]

        ident = tile("ident", [P, P], F32)
        make_identity(nc, ident[:])

        q_grp = tile("q_grp", [P, PACK * Q], BF16)
        weave(nc.vector.tensor_copy, q_grp, 0, q_raw, 0, Q)
        q_mx = quantise("q", q_grp, Q)
        scores = tile("scores", [P, T], F32)
        for c in range(4):
            acc = bank("a%d" % c, "A%d" % c, [P, HALF])
            h, c0 = divmod(c * HALF, KP)
            nc.tensor.matmul_mx(
                out=acc[:],
                lhsT=q_mx[0][:].bitcast(FP8X4),
                lhsT_scale=q_mx[1][:],
                rhs=k_codes[h][:, c0 : c0 + HALF].bitcast(FP8X4),
                rhs_scale=k_scales[:, c * HALF : (c + 1) * HALF],
                start=True,
                stop=True,
            )
            copy = nc.scalar.copy if c % 2 == 0 else nc.vector.tensor_copy
            copy(out=scores[:, c * HALF : (c + 1) * HALF], in_=acc[:])

        neg_r = tile("neg_r", [P, M], F32)
        neg_zb = tile("neg_zb", [P, 1], F32)
        neg_z = tile("neg_z", [P, 1], F32)
        listed = tile("listed", [P, I], F32)
        nc.vector.tensor_copy(listed[:], scores[:].indirect(offsets[:]))
        r_acc = bank("r", "A2", [P, M])
        pk_grp = [tile("pk_grp%d" % h, [P, PACK * HALF], BF16) for h in range(2)]
        for h in range(2):
            weave(nc.scalar.copy, pk_grp[h], 0, pk_raw[h], 0, HALF)
            pk_mx = quantise("pk%d" % h, pk_grp[h], HALF)
            product(r_acc[:, h * HALF : (h + 1) * HALF], q_mx, pk_mx, 0, HALF, True, True)
        neg_listed = tile("neg_listed", [P, I], F32, tag="pk_grp1")
        nc.vector.tensor_scalar(
            out=neg_listed[:], in0=listed[:], scalar1=-1.0, scalar2=None, op0=ALU.mult, op1=ALU.min, accum_out=neg_zb[:]
        )
        nc.vector.tensor_scalar(
            out=neg_r[:], in0=r_acc[:], scalar1=-1.0, scalar2=neg_zb[:], op0=ALU.mult, op1=ALU.min, accum_out=neg_z[:]
        )

        def value_half(name, raw, copy):
            grp = tile(name + "_grp", [P, PACK * HALF], BF16)
            weave(copy, grp, 0, raw, 0, HALF)
            return grp

        pv_grp = [value_half("pv0", pv_raw[0], nc.scalar.copy)]
        p = tile("p", [P, I], F32)
        x = tile("x", [P, M], F32)
        sums = tile("sums", [P, 3], F32)
        nc.scalar.activation(out=p[:, 0:HALF], in_=neg_listed[:, 0:HALF], func=ACT.Exp, scale=-1.0, bias=neg_z[:], accum_out=sums[:, 0:1])
        nc.scalar.activation(out=p[:, HALF:I], in_=neg_listed[:, HALF:I], func=ACT.Exp, scale=-1.0, bias=neg_z[:], accum_out=sums[:, 1:2])
        nc.scalar.activation(out=x[:], in_=neg_r[:], func=ACT.Exp, scale=-1.0, bias=neg_z[:], accum_out=sums[:, 2:3])
        pv_mx = [quantise("pv0", pv_grp[0], HALF)]
        for h in range(2):
            nc.vector.tensor_copy(placed[:].indirect(offsets[:, 16 * h : 16 * (h + 1)]), p[:, h * HALF : (h + 1) * HALF])
        sums_again = tile("sums_again", [P, 3], F32)
        total = tile("total", [P, 1], F32)
        nc.scalar.activation(out=sums_again[:], in_=sums[:], func=ACT.Copy, accum_out=total[:])
        inv = tile("inv", [P, 1], F32)
        nc.vector.reciprocal(out=inv[:], in_=total[:])

        factor_turned = bank("factor_turned", "R", [P, P])
        nc.tensor.transpose(factor_turned[:], factor_rows[:], ident[:])
        factor_cols = tile("factor_cols", [P, 12], F32)
        nc.scalar.copy(out=factor_cols[:], in_=factor_turned[:, 0:12])
        spread = []
        for g in range(3):
            sp = bank("spread%d" % g, "S%d" % g, [P, KP])
            for m in range(4):
                col = factor_cols[:, 4 * g + m : 4 * g + m + 1]
                nc.tensor.transpose(sp[:, m * P : (m + 1) * P], col.to_broadcast([P, P]), ident[:])
            spread.append(sp)

        pv_grp.append(value_half("pv1", pv_raw[1], nc.scalar.copy))
        v0_grp = tile("v0_grp", [P, PACK * E], BF16)
        for h in range(2):
            weave(nc.scalar.copy, v0_grp, h * HALF, v0_raw, h * HALF, (h + 1) * HALF)
        v1_grp = [value_half("v10", v1_raw[0], nc.scalar.copy)]

        def weights(name, src, sp, tag, grp):
            wb = tile(name + "_bf", [P, KP], BF16)
            nc.vector.scalar_tensor_tensor(
                out=wb[:],
                in0=src,
                scalar=inv[:],
                in1=sp[:],
                op0=ALU.mult,
                op1=ALU.mult,
            )
            pairs = wb[:].bitcast(F32)
            turned = bank(name + "_turned", tag, [P, 2, Q])
            for u in range(2):
                nc.tensor.transpose(turned[:, u, :], pairs[:, u : 2 * P : 2], ident[:])
            nc.scalar.copy(
                out=grp.bitcast(F32).rearrange("p (q u) -> p q u", u=2), in_=turned[:].rearrange("p u q -> p q u")
            )

        pv_mx.append(quantise("pv1", pv_grp[1], HALF))
        wu_grp = tile("wu_grp", [P, 3 * KP], BF16, tag="v1_raw0")
        weights("w0", placed[:, 0:KP], spread[0], "A2", wu_grp[:, 0:KP])
        weights("u", x[:], spread[2], "R", wu_grp[:, KP : 2 * KP])
        weights("w1", placed[:, KP:T], spread[1], "A3", wu_grp[:, 2 * KP : 3 * KP])
        v11_grp = tile("v11_grp", [P, PACK * HALF], BF16)
        weave(nc.scalar.copy, v11_grp, 0, v1_raw[1], 0, HALF)
        v0_mx = quantise("v0", v0_grp, E)
        accs = [bank("o%d" % h, "A%d" % h, [P, HALF]) for h in range(2)]
        w0_mx = quantise("w0", wu_grp[:, 0:KP], Q)
        for h in range(2):
            product(accs[h][:], w0_mx, v0_mx, h * HALF, (h + 1) * HALF, True, False)
        u_mx = quantise("u", wu_grp[:, KP : 2 * KP], Q)
        for h in range(2):
            product(accs[h][:], u_mx, pv_mx[h], 0, HALF, False, False)
        w1_mx = quantise("w1", wu_grp[:, 2 * KP : 3 * KP], Q)
        v1_mx = [quantise("v10", v1_grp[0], HALF, tag="v1_raw0"), quantise("v11", v11_grp, HALF)]
        for h in range(2):
            product(accs[h][:], w1_mx, v1_mx[h], 0, HALF, False, True)
            res = tile("res%d" % h, [P, HALF], F32)
            copy = nc.scalar.copy if h == 0 else nc.vector.tensor_copy
            copy(out=res[:], in_=accs[h][:])
            nc.sync.dma_start(out=out[:, h * HALF : (h + 1) * HALF], in_=res[:])
